import numpy as np
import ml_dtypes


def mxq(x, axis, fmt="e4m3"):
    dtype, down = {"e4m3": (ml_dtypes.float8_e4m3fn, 7), "e5m2": (ml_dtypes.float8_e5m2, 14)}[fmt]
    v = np.moveaxis(np.asarray(x, np.float32).astype(ml_dtypes.bfloat16).astype(np.float64), axis, -1)
    blocks = v.reshape(v.shape[:-1] + (-1, 32))
    amax = np.abs(blocks).max(-1, keepdims=True)
    byte = np.maximum(np.where(amax > 0, np.frexp(amax)[1] - 1 + 127, 0) - down, 1)
    scale = np.exp2(byte - 127.0)
    codes = (blocks / scale).astype(np.float32).astype(dtype).astype(np.float64)
    return np.moveaxis((codes * scale).reshape(v.shape), -1, axis)


WIDE = False


def mx_kscale(k):
    if not WIDE:
        return np.ones(k)
    levels = np.array([10, -10, 5, -5, 0])
    if k % 512:
        return np.exp2(np.random.permutation(np.resize(levels, k // 32))).repeat(32)
    a = np.empty((k // 512, 16))
    for p in range(k // 512):
        a[p, :8] = np.random.permutation(np.resize(levels, 8))
        for g in range(8):
            far = levels[np.abs(levels - a[p, g]) >= 10]
            a[p, g + 8] = far[np.random.randint(len(far))]
    return np.exp2(a.ravel()).repeat(32)


def f64(x):
    return np.asarray(x).astype(np.float64)


def striped(idx):
    return np.tile(np.asarray(idx).reshape(-1, 16).T, (8, 1)).astype(np.uint16)


def unstriped(offs):
    return offs[:16].T.reshape(-1).astype(np.int64)


B, N, T, D, DV, NQ = 1, 512, 1024, 512, 128, 128
NEW = 256


def setup_inputs():
    n = np.random.standard_normal
    idx = np.random.permutation(T)[:B * N]
    s = mx_kscale(D)[:, None]
    u = np.ones(T)
    u[idx] = mx_kscale(B * N)
    r = np.random.uniform(0.5, 2.0, T)
    k = n((D, T)) / s
    v = n((DV, T)) / (u * r)
    new = np.random.permutation(idx.reshape(B, N)[:, -NEW // B:].reshape(-1))
    return {
        "qT": (n((B, D, NQ)) * s * (0.80 / np.sqrt(D))).astype(np.float32),
        "kT": np.where(np.isin(np.arange(T), new)[None, :], n((D, T)), k).astype(np.float32),
        "vT": np.where(np.isin(np.arange(T), new)[None, :], n((DV, T)), v).astype(np.float32),
        "new_kT": k[:, new].astype(np.float32),
        "new_vT": v[:, new].astype(np.float32),
        "vs": np.tile(u * r, (128, 1)).astype(np.float32),
        "sink": (2.0 + 3.0 * n((B, NQ, 1))).astype(np.float32),
        "offs": striped(idx),
        "slots": striped(new),
    }


def reference(qT, kT, vT, new_kT, new_vT, vs, sink, offs, slots):
    idx = unstriped(offs)
    k = f64(kT)
    k[:, unstriped(slots)] = f64(new_kT)
    v = f64(vT)
    v[:, unstriped(slots)] = f64(new_vT)
    pick = lambda x: x[:, idx].reshape(x.shape[0], B, N).transpose(1, 0, 2)
    q = f64(qT)
    score = mxq(q, 1, "e4m3").transpose(0, 2, 1) @ mxq(pick(k), 1, "e4m3")
    m = np.maximum(score.max(-1, keepdims=True), f64(sink))
    p = np.exp(score - m)
    total = p.sum(-1, keepdims=True) + np.exp(f64(sink) - m)
    w = p * pick(f64(vs))[:, :1, :]
    y = mxq(w, 2, "e4m3") @ mxq(pick(v).transpose(0, 2, 1), 1, "e4m3")
    y = y / total
    return y

@@ -1,0 +1,149 @@
+from contextlib import ExitStack
+
+import concourse.mybir as mybir
+from concourse.masks import make_identity
+
+F32 = mybir.dt.float32
+BF16 = mybir.dt.bfloat16
+U32 = mybir.dt.uint32
+U16 = mybir.dt.uint16
+U8 = mybir.dt.uint8
+FP8X4 = mybir.dt.float8_e4m3fn_x4
+MULT = mybir.AluOpType.mult
+ADD = mybir.AluOpType.add
+MAX = mybir.AluOpType.max
+MIN = mybir.AluOpType.min
+EXP = mybir.ActivationFunctionType.Exp
+COPY = mybir.ActivationFunctionType.Copy
+AXIS_X = mybir.AxisListType.X
+
+P = 128
+N, T, D, DV, NQ, NEW = 512, 1024, 512, 128, 128, 256
+FLOPS = 2 * NQ * N * (D + DV)
+
+
+def tile_attend_kv_append256_sink_kernel(tc, qT, kT, vT, new_kT, new_vT, vs, sink, offs, slots, out):
+    nc = tc.nc
+    with ExitStack() as ctx:
+        held = ctx.enter_context(tc.tile_pool(name="held", bufs=1))
+        psum = ctx.enter_context(tc.psum_pool(name="psum", bufs=1))
+
+        slots_sb = held.tile([P, NEW // 16], U16, name="slots_sb")
+        offs_sb = held.tile([P, N // 16], U16, name="offs_sb")
+        newv = held.tile([P, NEW], F32, name="newv")
+        vpool = held.tile([P, T], F32, name="vpool")
+        newk = [held.tile([P, NEW], F32, name=f"newk{t}") for t in range(4)]
+        kpool = [held.tile([P, T], F32, name=f"kpool{t}") for t in range(4)]
+        q_raw = held.tile([P, 4, NQ], F32, name="q_raw")
+        vs_sb = held.tile([P, T], F32, name="vs_sb")
+        sink_sb = held.tile([P, 1], F32, name="sink_sb")
+
+        kT_v = kT.rearrange("(p t) n -> p t n", t=4)
+        newk_v = new_kT.rearrange("(p t) n -> p t n", t=4)
+        nc.sync.dma_start(slots_sb[:], slots)
+        nc.sync.dma_start(newv[:], new_vT)
+        nc.sync.dma_start(vpool[:], vT)
+        nc.sync.dma_start(offs_sb[:], offs)
+        for t in range(4):
+            nc.sync.dma_start(newk[t][:], newk_v[:, t, :])
+            nc.sync.dma_start(kpool[t][:], kT_v[:, t, :])
+            if t == 1:
+                nc.sync.dma_start(q_raw[:], qT.rearrange("b (p t) q -> p (b t) q", t=4))
+        nc.sync.dma_start(vs_sb[:], vs)
+        nc.scalar.dma_start(sink_sb[:], sink.rearrange("b q o -> (b q) o"))
+
+        ident_f = held.tile([P, P], F32, name="ident_f")
+        make_identity(nc, ident_f[:])
+        ident_b = held.tile([P, P], BF16, name="ident_b")
+        make_identity(nc, ident_b[:])
+        warm = held.tile([P, 1], F32, name="warm")
+        nc.gpsimd.memset(warm[:], 0.0)
+        nc.scalar.activation(warm[:], warm[:], EXP)
+
+        nc.vector.tensor_copy(vpool[:].indirect(slots_sb[:]), newv[:])
+        vpool_b = held.tile([P, T], BF16, name="vpool_b")
+        nc.scalar.copy(vpool_b[:], vpool[:])
+
+        kpair = [held.tile([P, 2 * T], BF16, name=f"kpair{u}", align_bytes=64) for u in range(2)]
+        for t in range(4):
+            nc.vector.tensor_copy(kpool[t][:].indirect(slots_sb[:]), newk[t][:])
+            nc.scalar.copy(kpair[t // 2][:].rearrange("p (n j) -> p n j", j=2)[:, :, t % 2], kpool[t][:])
+
+        q_b = held.tile([P, NQ, 4], BF16, name="q_b", align_bytes=64)
+        nc.scalar.copy(q_b[:], q_raw[:].rearrange("p t q -> p q t"))
+        q_c = held.tile([P, NQ], U32, name="q_c", align_bytes=64)
+        q_s = held.tile([P, NQ], U8, name="q_s", align_bytes=64)
+        nc.vector.quantize_mx(out=q_c[:].bitcast(FP8X4), scales=q_s[:], in_=q_b[:].rearrange("p q t -> p (q t)"))
+
+        k_g = held.tile([P, N * 4], BF16, name="k_g", align_bytes=64)
+        k_g32 = k_g[:].bitcast(U32).rearrange("p (n u) -> p n u", u=2)
+        for u in range(2):
+            nc.vector.tensor_copy(k_g32[:, :, u], kpair[u][:].bitcast(U32).indirect(offs_sb[:]))
+        k_c = held.tile([P, N], U32, name="k_c", align_bytes=64)
+        k_s = held.tile([P, N], U8, name="k_s", align_bytes=64)
+        nc.vector.quantize_mx(out=k_c[:].bitcast(FP8X4), scales=k_s[:], in_=k_g[:])
+
+        score = psum.tile([P, N], F32, name="score")
+        nc.tensor.matmul_mx(score[:], lhsT=q_c[:].bitcast(FP8X4), lhsT_scale=q_s[:], rhs=k_c[:].bitcast(FP8X4), rhs_scale=k_s[:], start=True, stop=True)
+
+        v_g = held.tile([P, N, 2], BF16, name="v_g", align_bytes=64)
+        nc.scalar.activation(v_g[:, :, 0], vpool_b[:].indirect(offs_sb[:]), COPY)
+        v_ps = psum.tile([P, 4, DV], BF16, name="v_ps")
+        for t in range(4):
+            nc.tensor.transpose(v_ps[:, t, :], v_g[:, t::4, 0], ident_b[:])
+        v_b = held.tile([P, DV, 4], BF16, name="v_b", align_bytes=64)
+        nc.scalar.copy(v_b[:], v_ps[:].rearrange("p t e -> p e t"))
+
+        negsink = held.tile([P, 1], F32, name="negsink")
+        nc.vector.tensor_scalar(negsink[:], sink_sb[:], -1.0, None, op0=MULT)
+        negmax = held.tile([P, 1], F32, name="negmax")
+        nc.vector.tensor_reduce(negmax[:], score[:], axis=AXIS_X, op=MAX, negate=True)
+        negm = held.tile([P, 1], F32, name="negm")
+        nc.vector.tensor_tensor(negm[:], negmax[:], negsink[:], MIN)
+
+        p_sb = held.tile([P, 4, P], F32, name="p_sb")
+        l_ab = held.tile([P, 2], F32, name="l_ab")
+        score_v = score[:].rearrange("q (s t) -> q t s", t=4)
+        for h in range(2):
+            nc.scalar.activation(p_sb[:, 2 * h : 2 * h + 2, :], score_v[:, 2 * h : 2 * h + 2, :], EXP, bias=negm[:], accum_out=l_ab[:, h : h + 1])
+
+        vs_g = held.tile([P, N], F32, name="vs_g")
+        nc.vector.tensor_copy(vs_g[:], vs_sb[:].indirect(offs_sb[:]))
+        vs_ps = psum.tile([P, 4, P], F32, name="vs_ps")
+        for t in range(4):
+            nc.tensor.transpose(vs_ps[:, t, :], vs_g[:, t::4], ident_f[:])
+        vs_col = held.tile([P, 4], F32, name="vs_col")
+        nc.vector.tensor_copy(vs_col[:], vs_ps[:, :, 0])
+
+        v_c = held.tile([P, DV], U32, name="v_c", align_bytes=64)
+        v_s = held.tile([P, DV], U8, name="v_s", align_bytes=64)
+        nc.vector.quantize_mx(out=v_c[:].bitcast(FP8X4), scales=v_s[:], in_=v_b[:].rearrange("p e t -> p (e t)"))
+
+        w_b = held.tile([P, NQ, 4], BF16, name="w_b", align_bytes=64)
+        for h in range(2):
+            p_ps = psum.tile([P, 2, NQ], F32, name=f"p_ps{h}")
+            for t in range(2):
+                nc.tensor.transpose(p_ps[:, t, :], p_sb[:, 2 * h + t, :], ident_f[:])
+            nc.vector.tensor_tensor(
+                w_b[:, :, 2 * h : 2 * h + 2],
+                p_ps[:].rearrange("s t q -> s q t"),
+                vs_col[:, 2 * h : 2 * h + 2].unsqueeze(1).to_broadcast([P, NQ, 2]),
+                MULT,
+            )
+        w_c = held.tile([P, NQ], U32, name="w_c", align_bytes=64)
+        w_s = held.tile([P, NQ], U8, name="w_s", align_bytes=64)
+        nc.vector.quantize_mx(out=w_c[:].bitcast(FP8X4), scales=w_s[:], in_=w_b[:].rearrange("p q t -> p (q t)"))
+
+        y_ps = psum.tile([P, DV], F32, name="y_ps")
+        nc.tensor.matmul_mx(y_ps[:], lhsT=w_c[:].bitcast(FP8X4), lhsT_scale=w_s[:], rhs=v_c[:].bitcast(FP8X4), rhs_scale=v_s[:], start=True, stop=True)
+
+        e_sink = held.tile([P, 1], F32, name="e_sink")
+        nc.scalar.activation(e_sink[:], sink_sb[:], EXP, bias=negm[:])
+        l_0 = held.tile([P, 1], F32, name="l_0")
+        nc.vector.scalar_tensor_tensor(l_0[:], l_ab[:, 0:1], e_sink[:], l_ab[:, 1:2], ADD, ADD)
+        r_l = held.tile([P, 1], F32, name="r_l")
+        nc.vector.reciprocal(r_l[:], l_0[:])
+
+        y_sb = held.tile([P, DV], F32, name="y_sb")
+        nc.vector.tensor_scalar(y_sb[:], y_ps[:], r_l[:], None, op0=MULT)
+        nc.sync.dma_start(out.rearrange("b q e -> (b q) e"), y_sb[:])

@@ -30,25 +30,25 @@ def tile_attend_kv_append256_sink_kernel(tc, qT, kT, vT, new_kT, new_vT, vs, sin
 
         slots_sb = held.tile([P, NEW // 16], U16, name="slots_sb")
         offs_sb = held.tile([P, N // 16], U16, name="offs_sb")
-        newv = held.tile([P, NEW], F32, name="newv")
+        newv = held.tile([P, NEW], F32, name="newv", tag="ring", align_bytes=64)
         vpool = held.tile([P, T], F32, name="vpool")
         newk = [held.tile([P, NEW], F32, name=f"newk{t}") for t in range(4)]
-        kpool = [held.tile([P, T], F32, name=f"kpool{t}") for t in range(4)]
+        kpool = [held.tile([P, T], F32, name=f"kpool{t}", tag=f"kpool{t}", align_bytes=64) for t in range(4)]
         q_raw = held.tile([P, 4, NQ], F32, name="q_raw")
         vs_sb = held.tile([P, T], F32, name="vs_sb")
         sink_sb = held.tile([P, 1], F32, name="sink_sb")
 
         kT_v = kT.rearrange("(p t) n -> p t n", t=4)
         newk_v = new_kT.rearrange("(p t) n -> p t n", t=4)
-        nc.sync.dma_start(slots_sb[:], slots)
+        for t in range(4):
+            nc.sync.dma_start(kpool[t][:], kT_v[:, t, :])
+            nc.sync.dma_start(newk[t][:], newk_v[:, t, :])
+            if t == 0:
+                nc.sync.dma_start(slots_sb[:], slots)
         nc.sync.dma_start(newv[:], new_vT)
         nc.sync.dma_start(vpool[:], vT)
+        nc.sync.dma_start(q_raw[:], qT.rearrange("b (p t) q -> p (b t) q", t=4))
         nc.sync.dma_start(offs_sb[:], offs)
-        for t in range(4):
-            nc.sync.dma_start(newk[t][:], newk_v[:, t, :])
-            nc.sync.dma_start(kpool[t][:], kT_v[:, t, :])
-            if t == 1:
-                nc.sync.dma_start(q_raw[:], qT.rearrange("b (p t) q -> p (b t) q", t=4))
         nc.sync.dma_start(vs_sb[:], vs)
         nc.scalar.dma_start(sink_sb[:], sink.rearrange("b q o -> (b q) o"))
 
@@ -60,25 +60,24 @@ def tile_attend_kv_append256_sink_kernel(tc, qT, kT, vT, new_kT, new_vT, vs, sin
         nc.gpsimd.memset(warm[:], 0.0)
         nc.scalar.activation(warm[:], warm[:], EXP)
 
-        nc.vector.tensor_copy(vpool[:].indirect(slots_sb[:]), newv[:])
-        vpool_b = held.tile([P, T], BF16, name="vpool_b")
-        nc.scalar.copy(vpool_b[:], vpool[:])
-
-        kpair = [held.tile([P, 2 * T], BF16, name=f"kpair{u}", align_bytes=64) for u in range(2)]
+        kpair = [held.tile([P, 2 * T], BF16, name=f"kpair{u}", tag=f"kpair{u}", align_bytes=64) for u in range(2)]
         for t in range(4):
             nc.vector.tensor_copy(kpool[t][:].indirect(slots_sb[:]), newk[t][:])
             nc.scalar.copy(kpair[t // 2][:].rearrange("p (n j) -> p n j", j=2)[:, :, t % 2], kpool[t][:])
 
-        q_b = held.tile([P, NQ, 4], BF16, name="q_b", align_bytes=64)
+        nc.vector.tensor_copy(vpool[:].indirect(slots_sb[:]), newv[:])
+        q_b = held.tile([P, NQ, 4], BF16, name="q_b", tag="kpool3", align_bytes=64)
         nc.scalar.copy(q_b[:], q_raw[:].rearrange("p t q -> p q t"))
-        q_c = held.tile([P, NQ], U32, name="q_c", align_bytes=64)
-        q_s = held.tile([P, NQ], U8, name="q_s", align_bytes=64)
-        nc.vector.quantize_mx(out=q_c[:].bitcast(FP8X4), scales=q_s[:], in_=q_b[:].rearrange("p q t -> p (q t)"))
+        vpool_b = held.tile([P, T], BF16, name="vpool_b")
+        nc.scalar.copy(vpool_b[:], vpool[:])
 
-        k_g = held.tile([P, N * 4], BF16, name="k_g", align_bytes=64)
+        k_g = held.tile([P, N * 4], BF16, name="k_g", tag="ring", align_bytes=64)
         k_g32 = k_g[:].bitcast(U32).rearrange("p (n u) -> p n u", u=2)
         for u in range(2):
             nc.vector.tensor_copy(k_g32[:, :, u], kpair[u][:].bitcast(U32).indirect(offs_sb[:]))
+        q_c = held.tile([P, NQ], U32, name="q_c", tag="kpair1", align_bytes=64)
+        q_s = held.tile([P, NQ], U8, name="q_s", align_bytes=64)
+        nc.vector.quantize_mx(out=q_c[:].bitcast(FP8X4), scales=q_s[:], in_=q_b[:].rearrange("p q t -> p (q t)"))
         k_c = held.tile([P, N], U32, name="k_c", align_bytes=64)
         k_s = held.tile([P, N], U8, name="k_s", align_bytes=64)
         nc.vector.quantize_mx(out=k_c[:].bitcast(FP8X4), scales=k_s[:], in_=k_g[:])
@@ -95,11 +94,18 @@ def tile_attend_kv_append256_sink_kernel(tc, qT, kT, vT, new_kT, new_vT, vs, sin
         nc.scalar.copy(v_b[:], v_ps[:].rearrange("p t e -> p e t"))
 
         negsink = held.tile([P, 1], F32, name="negsink")
-        nc.vector.tensor_scalar(negsink[:], sink_sb[:], -1.0, None, op0=MULT)
-        negmax = held.tile([P, 1], F32, name="negmax")
-        nc.vector.tensor_reduce(negmax[:], score[:], axis=AXIS_X, op=MAX, negate=True)
+        nc.gpsimd.tensor_scalar(negsink[:], sink_sb[:], -1.0, 0.0, op0=MULT, op1=ADD)
+        vs_g = held.tile([P, N], F32, name="vs_g", tag="ring", align_bytes=64)
+        nc.vector.tensor_copy(vs_g[:], vs_sb[:].indirect(offs_sb[:]))
+        vs_ps = psum.tile([P, 4, P], F32, name="vs_ps")
+        for t in range(4):
+            nc.tensor.transpose(vs_ps[:, t, :], vs_g[:, t::4], ident_f[:])
+
         negm = held.tile([P, 1], F32, name="negm")
-        nc.vector.tensor_tensor(negm[:], negmax[:], negsink[:], MIN)
+        neg_score = held.tile([P, N], F32, name="neg_score")
+        nc.vector.tensor_scalar(neg_score[:], score[:], -1.0, negsink[:], op0=MULT, op1=MIN, accum_out=negm[:])
+        vs_col = held.tile([P, 4], F32, name="vs_col")
+        nc.vector.tensor_copy(vs_col[:], vs_ps[:, :, 0])
 
         p_sb = held.tile([P, 4, P], F32, name="p_sb")
         l_ab = held.tile([P, 2], F32, name="l_ab")
@@ -107,32 +113,27 @@ def tile_attend_kv_append256_sink_kernel(tc, qT, kT, vT, new_kT, new_vT, vs, sin
         for h in range(2):
             nc.scalar.activation(p_sb[:, 2 * h : 2 * h + 2, :], score_v[:, 2 * h : 2 * h + 2, :], EXP, bias=negm[:], accum_out=l_ab[:, h : h + 1])
 
-        vs_g = held.tile([P, N], F32, name="vs_g")
-        nc.vector.tensor_copy(vs_g[:], vs_sb[:].indirect(offs_sb[:]))
-        vs_ps = psum.tile([P, 4, P], F32, name="vs_ps")
-        for t in range(4):
-            nc.tensor.transpose(vs_ps[:, t, :], vs_g[:, t::4], ident_f[:])
-        vs_col = held.tile([P, 4], F32, name="vs_col")
-        nc.vector.tensor_copy(vs_col[:], vs_ps[:, :, 0])
-
         v_c = held.tile([P, DV], U32, name="v_c", align_bytes=64)
         v_s = held.tile([P, DV], U8, name="v_s", align_bytes=64)
         nc.vector.quantize_mx(out=v_c[:].bitcast(FP8X4), scales=v_s[:], in_=v_b[:].rearrange("p e t -> p (e t)"))
 
         w_b = held.tile([P, NQ, 4], BF16, name="w_b", align_bytes=64)
+        w_c = held.tile([P, NQ], U32, name="w_c", align_bytes=64)
+        w_s = held.tile([P, NQ], U8, name="w_s", align_bytes=64)
         for h in range(2):
             p_ps = psum.tile([P, 2, NQ], F32, name=f"p_ps{h}")
             for t in range(2):
                 nc.tensor.transpose(p_ps[:, t, :], p_sb[:, 2 * h + t, :], ident_f[:])
-            nc.vector.tensor_tensor(
-                w_b[:, :, 2 * h : 2 * h + 2],
-                p_ps[:].rearrange("s t q -> s q t"),
-                vs_col[:, 2 * h : 2 * h + 2].unsqueeze(1).to_broadcast([P, NQ, 2]),
-                MULT,
-            )
-        w_c = held.tile([P, NQ], U32, name="w_c", align_bytes=64)
-        w_s = held.tile([P, NQ], U8, name="w_s", align_bytes=64)
-        nc.vector.quantize_mx(out=w_c[:].bitcast(FP8X4), scales=w_s[:], in_=w_b[:].rearrange("p q t -> p (q t)"))
+            for c in ((slice(0, NQ),), (slice(0, NQ // 2), slice(NQ // 2, NQ)))[h]:
+                nc.vector.tensor_tensor(
+                    w_b[:, c, 2 * h : 2 * h + 2],
+                    p_ps[:, :, c].rearrange("s t q -> s q t"),
+                    vs_col[:, 2 * h : 2 * h + 2].unsqueeze(1).to_broadcast([P, c.stop - c.start, 2]),
+                    MULT,
+                )
+        for h in range(2):
+            c = slice(h * NQ // 2, (h + 1) * NQ // 2)
+            nc.vector.quantize_mx(out=w_c[:, c].bitcast(FP8X4), scales=w_s[:, c], in_=w_b[:, c, :].rearrange("p q t -> p (q t)"))
 
         y_ps = psum.tile([P, DV], F32, name="y_ps")
         nc.tensor.matmul_mx(y_ps[:], lhsT=w_c[:].bitcast(FP8X4), lhsT_scale=w_s[:], rhs=v_c[:].bitcast(FP8X4), rhs_scale=v_s[:], start=True, stop=True)

@@ -32,7 +32,9 @@ def tile_attend_kv_append256_sink_kernel(tc, qT, kT, vT, new_kT, new_vT, vs, sin
         offs_sb = held.tile([P, N // 16], U16, name="offs_sb")
         newv = held.tile([P, NEW], F32, name="newv", tag="ring", align_bytes=64)
         vpool = held.tile([P, T], F32, name="vpool")
-        newk = [held.tile([P, NEW], F32, name=f"newk{t}") for t in range(4)]
+        newk01 = [held.tile([P, NEW], F32, name=f"newk{t}") for t in range(2)]
+        newk23 = held.tile([P, 2, NEW], F32, name="newk23")
+        newk = [newk01[0][:], newk01[1][:], newk23[:, 0, :], newk23[:, 1, :]]
         kpool = [held.tile([P, T], F32, name=f"kpool{t}", tag=f"kpool{t}", align_bytes=64) for t in range(4)]
         q_raw = held.tile([P, 4, NQ], F32, name="q_raw")
         vs_sb = held.tile([P, T], F32, name="vs_sb")
@@ -42,7 +44,10 @@ def tile_attend_kv_append256_sink_kernel(tc, qT, kT, vT, new_kT, new_vT, vs, sin
         newk_v = new_kT.rearrange("(p t) n -> p t n", t=4)
         for t in range(4):
             nc.sync.dma_start(kpool[t][:], kT_v[:, t, :])
-            nc.sync.dma_start(newk[t][:], newk_v[:, t, :])
+            if t < 2:
+                nc.sync.dma_start(newk[t], newk_v[:, t, :])
+            if t == 2:
+                nc.sync.dma_start(newk23[:], newk_v[:, 2:, :])
             if t == 0:
                 nc.sync.dma_start(slots_sb[:], slots)
         nc.sync.dma_start(newv[:], new_vT)
@@ -54,15 +59,13 @@ def tile_attend_kv_append256_sink_kernel(tc, qT, kT, vT, new_kT, new_vT, vs, sin
 
         ident_f = held.tile([P, P], F32, name="ident_f")
         make_identity(nc, ident_f[:])
-        ident_b = held.tile([P, P], BF16, name="ident_b")
-        make_identity(nc, ident_b[:])
         warm = held.tile([P, 1], F32, name="warm")
         nc.gpsimd.memset(warm[:], 0.0)
         nc.scalar.activation(warm[:], warm[:], EXP)
 
         kpair = [held.tile([P, 2 * T], BF16, name=f"kpair{u}", tag=f"kpair{u}", align_bytes=64) for u in range(2)]
         for t in range(4):
-            nc.vector.tensor_copy(kpool[t][:].indirect(slots_sb[:]), newk[t][:])
+            nc.vector.tensor_copy(kpool[t][:].indirect(slots_sb[:]), newk[t])
             nc.scalar.copy(kpair[t // 2][:].rearrange("p (n j) -> p n j", j=2)[:, :, t % 2], kpool[t][:])
 
         nc.vector.tensor_copy(vpool[:].indirect(slots_sb[:]), newv[:])
@@ -75,6 +78,10 @@ def tile_attend_kv_append256_sink_kernel(tc, qT, kT, vT, new_kT, new_vT, vs, sin
         k_g32 = k_g[:].bitcast(U32).rearrange("p (n u) -> p n u", u=2)
         for u in range(2):
             nc.vector.tensor_copy(k_g32[:, :, u], kpair[u][:].bitcast(U32).indirect(offs_sb[:]))
+        warm_ps = psum.tile([P, P], F32, name="warm_ps")
+        for i in range(18):
+            src = kpair[1] if i == 0 else kpair[0]
+            nc.tensor.transpose(warm_ps[:], src[:, (i % 8) * 2 * P : (i % 8 + 1) * 2 * P].bitcast(F32), ident_f[:])
         q_c = held.tile([P, NQ], U32, name="q_c", tag="kpair1", align_bytes=64)
         q_s = held.tile([P, NQ], U8, name="q_s", align_bytes=64)
         nc.vector.quantize_mx(out=q_c[:].bitcast(FP8X4), scales=q_s[:], in_=q_b[:].rearrange("p q t -> p (q t)"))
@@ -85,13 +92,13 @@ def tile_attend_kv_append256_sink_kernel(tc, qT, kT, vT, new_kT, new_vT, vs, sin
         score = psum.tile([P, N], F32, name="score")
         nc.tensor.matmul_mx(score[:], lhsT=q_c[:].bitcast(FP8X4), lhsT_scale=q_s[:], rhs=k_c[:].bitcast(FP8X4), rhs_scale=k_s[:], start=True, stop=True)
 
-        v_g = held.tile([P, N, 2], BF16, name="v_g", align_bytes=64)
-        nc.scalar.activation(v_g[:, :, 0], vpool_b[:].indirect(offs_sb[:]), COPY)
-        v_ps = psum.tile([P, 4, DV], BF16, name="v_ps")
-        for t in range(4):
-            nc.tensor.transpose(v_ps[:, t, :], v_g[:, t::4, 0], ident_b[:])
-        v_b = held.tile([P, DV, 4], BF16, name="v_b", align_bytes=64)
-        nc.scalar.copy(v_b[:], v_ps[:].rearrange("p t e -> p e t"))
+        v_g = held.tile([P, N], BF16, name="v_g", align_bytes=64)
+        nc.scalar.activation(v_g[:].rearrange("p (u s j) -> p s u j", u=2, j=2), vpool_b[:].indirect(offs_sb[:]), COPY)
+        v_ps = psum.tile([P, 2, DV], F32, name="v_ps")
+        for u in range(2):
+            nc.tensor.transpose(v_ps[:, u, :], v_g[:, u * (N // 2) : (u + 1) * (N // 2)].bitcast(F32), ident_f[:])
+        v_b = held.tile([P, DV * 4], BF16, name="v_b", align_bytes=64)
+        nc.scalar.copy(v_b[:].bitcast(F32).rearrange("p (e u) -> p e u", u=2), v_ps[:].rearrange("p u e -> p e u"))
 
         negsink = held.tile([P, 1], F32, name="negsink")
         nc.gpsimd.tensor_scalar(negsink[:], sink_sb[:], -1.0, 0.0, op0=MULT, op1=ADD)
@@ -115,7 +122,7 @@ def tile_attend_kv_append256_sink_kernel(tc, qT, kT, vT, new_kT, new_vT, vs, sin
 
         v_c = held.tile([P, DV], U32, name="v_c", align_bytes=64)
         v_s = held.tile([P, DV], U8, name="v_s", align_bytes=64)
-        nc.vector.quantize_mx(out=v_c[:].bitcast(FP8X4), scales=v_s[:], in_=v_b[:].rearrange("p e t -> p (e t)"))
+        nc.vector.quantize_mx(out=v_c[:].bitcast(FP8X4), scales=v_s[:], in_=v_b[:])
 
         w_b = held.tile([P, NQ, 4], BF16, name="w_b", align_bytes=64)
         w_c = held.tile([P, NQ], U32, name="w_c", align_bytes=64)

@@ -78,10 +78,6 @@ def tile_attend_kv_append256_sink_kernel(tc, qT, kT, vT, new_kT, new_vT, vs, sin
         k_g32 = k_g[:].bitcast(U32).rearrange("p (n u) -> p n u", u=2)
         for u in range(2):
             nc.vector.tensor_copy(k_g32[:, :, u], kpair[u][:].bitcast(U32).indirect(offs_sb[:]))
-        warm_ps = psum.tile([P, P], F32, name="warm_ps")
-        for i in range(18):
-            src = kpair[1] if i == 0 else kpair[0]
-            nc.tensor.transpose(warm_ps[:], src[:, (i % 8) * 2 * P : (i % 8 + 1) * 2 * P].bitcast(F32), ident_f[:])
         q_c = held.tile([P, NQ], U32, name="q_c", tag="kpair1", align_bytes=64)
         q_s = held.tile([P, NQ], U8, name="q_s", align_bytes=64)
         nc.vector.quantize_mx(out=q_c[:].bitcast(FP8X4), scales=q_s[:], in_=q_b[:].rearrange("p q t -> p (q t)"))

from contextlib import ExitStack

import concourse.mybir as mybir
from concourse.masks import make_identity

F32 = mybir.dt.float32
BF16 = mybir.dt.bfloat16
U32 = mybir.dt.uint32
U16 = mybir.dt.uint16
U8 = mybir.dt.uint8
FP8X4 = mybir.dt.float8_e4m3fn_x4
MULT = mybir.AluOpType.mult
ADD = mybir.AluOpType.add
MAX = mybir.AluOpType.max
MIN = mybir.AluOpType.min
EXP = mybir.ActivationFunctionType.Exp
COPY = mybir.ActivationFunctionType.Copy
AXIS_X = mybir.AxisListType.X

P = 128
N, T, D, DV, NQ, NEW = 512, 1024, 512, 128, 128, 256
FLOPS = 2 * NQ * N * (D + DV)


def tile_attend_kv_append256_sink_kernel(tc, qT, kT, vT, new_kT, new_vT, vs, sink, offs, slots, out):
    nc = tc.nc
    with ExitStack() as ctx:
        held = ctx.enter_context(tc.tile_pool(name="held", bufs=1))
        psum = ctx.enter_context(tc.psum_pool(name="psum", bufs=1))

        slots_sb = held.tile([P, NEW // 16], U16, name="slots_sb")
        offs_sb = held.tile([P, N // 16], U16, name="offs_sb")
        newv = held.tile([P, NEW], F32, name="newv", tag="ring", align_bytes=64)
        vpool = held.tile([P, T], F32, name="vpool")
        newk01 = [held.tile([P, NEW], F32, name=f"newk{t}") for t in range(2)]
        newk23 = held.tile([P, 2, NEW], F32, name="newk23")
        newk = [newk01[0][:], newk01[1][:], newk23[:, 0, :], newk23[:, 1, :]]
        kpool = [held.tile([P, T], F32, name=f"kpool{t}", tag=f"kpool{t}", align_bytes=64) for t in range(4)]
        q_raw = held.tile([P, 4, NQ], F32, name="q_raw")
        vs_sb = held.tile([P, T], F32, name="vs_sb")
        sink_sb = held.tile([P, 1], F32, name="sink_sb")

        kT_v = kT.rearrange("(p t) n -> p t n", t=4)
        newk_v = new_kT.rearrange("(p t) n -> p t n", t=4)
        for t in range(4):
            nc.sync.dma_start(kpool[t][:], kT_v[:, t, :])
            if t < 2:
                nc.sync.dma_start(newk[t], newk_v[:, t, :])
            if t == 2:
                nc.sync.dma_start(newk23[:], newk_v[:, 2:, :])
            if t == 0:
                nc.sync.dma_start(slots_sb[:], slots)
        nc.sync.dma_start(newv[:], new_vT)
        nc.sync.dma_start(vpool[:], vT)
        nc.sync.dma_start(q_raw[:], qT.rearrange("b (p t) q -> p (b t) q", t=4))
        nc.sync.dma_start(offs_sb[:], offs)
        nc.sync.dma_start(vs_sb[:], vs)
        nc.scalar.dma_start(sink_sb[:], sink.rearrange("b q o -> (b q) o"))

        ident_f = held.tile([P, P], F32, name="ident_f")
        make_identity(nc, ident_f[:])
        warm = held.tile([P, 1], F32, name="warm")
        nc.gpsimd.memset(warm[:], 0.0)
        nc.scalar.activation(warm[:], warm[:], EXP)

        kpair = [held.tile([P, 2 * T], BF16, name=f"kpair{u}", tag=f"kpair{u}", align_bytes=64) for u in range(2)]
        for t in range(4):
            nc.vector.tensor_copy(kpool[t][:].indirect(slots_sb[:]), newk[t])
            nc.scalar.copy(kpair[t // 2][:].rearrange("p (n j) -> p n j", j=2)[:, :, t % 2], kpool[t][:])

        nc.vector.tensor_copy(vpool[:].indirect(slots_sb[:]), newv[:])
        q_b = held.tile([P, NQ, 4], BF16, name="q_b", tag="kpool3", align_bytes=64)
        nc.scalar.copy(q_b[:], q_raw[:].rearrange("p t q -> p q t"))
        vpool_b = held.tile([P, T], BF16, name="vpool_b")
        nc.scalar.copy(vpool_b[:], vpool[:])

        k_g = held.tile([P, N * 4], BF16, name="k_g", tag="ring", align_bytes=64)
        k_g32 = k_g[:].bitcast(U32).rearrange("p (n u) -> p n u", u=2)
        for u in range(2):
            nc.vector.tensor_copy(k_g32[:, :, u], kpair[u][:].bitcast(U32).indirect(offs_sb[:]))
        q_c = held.tile([P, NQ], U32, name="q_c", tag="kpair1", align_bytes=64)
        q_s = held.tile([P, NQ], U8, name="q_s", align_bytes=64)
        nc.vector.quantize_mx(out=q_c[:].bitcast(FP8X4), scales=q_s[:], in_=q_b[:].rearrange("p q t -> p (q t)"))
        k_c = held.tile([P, N], U32, name="k_c", align_bytes=64)
        k_s = held.tile([P, N], U8, name="k_s", align_bytes=64)
        nc.vector.quantize_mx(out=k_c[:].bitcast(FP8X4), scales=k_s[:], in_=k_g[:])

        score = psum.tile([P, N], F32, name="score")
        nc.tensor.matmul_mx(score[:], lhsT=q_c[:].bitcast(FP8X4), lhsT_scale=q_s[:], rhs=k_c[:].bitcast(FP8X4), rhs_scale=k_s[:], start=True, stop=True)

        v_g = held.tile([P, N], BF16, name="v_g", align_bytes=64)
        nc.scalar.activation(v_g[:].rearrange("p (u s j) -> p s u j", u=2, j=2), vpool_b[:].indirect(offs_sb[:]), COPY)
        v_ps = psum.tile([P, 2, DV], F32, name="v_ps")
        for u in range(2):
            nc.tensor.transpose(v_ps[:, u, :], v_g[:, u * (N // 2) : (u + 1) * (N // 2)].bitcast(F32), ident_f[:])
        v_b = held.tile([P, DV * 4], BF16, name="v_b", align_bytes=64)
        nc.scalar.copy(v_b[:].bitcast(F32).rearrange("p (e u) -> p e u", u=2), v_ps[:].rearrange("p u e -> p e u"))

        negsink = held.tile([P, 1], F32, name="negsink")
        nc.gpsimd.tensor_scalar(negsink[:], sink_sb[:], -1.0, 0.0, op0=MULT, op1=ADD)
        vs_g = held.tile([P, N], F32, name="vs_g", tag="ring", align_bytes=64)
        nc.vector.tensor_copy(vs_g[:], vs_sb[:].indirect(offs_sb[:]))
        vs_ps = psum.tile([P, 4, P], F32, name="vs_ps")
        for t in range(4):
            nc.tensor.transpose(vs_ps[:, t, :], vs_g[:, t::4], ident_f[:])

        negm = held.tile([P, 1], F32, name="negm")
        neg_score = held.tile([P, N], F32, name="neg_score")
        nc.vector.tensor_scalar(neg_score[:], score[:], -1.0, negsink[:], op0=MULT, op1=MIN, accum_out=negm[:])
        vs_col = held.tile([P, 4], F32, name="vs_col")
        nc.vector.tensor_copy(vs_col[:], vs_ps[:, :, 0])

        p_sb = held.tile([P, 4, P], F32, name="p_sb")
        l_ab = held.tile([P, 2], F32, name="l_ab")
        score_v = score[:].rearrange("q (s t) -> q t s", t=4)
        for h in range(2):
            nc.scalar.activation(p_sb[:, 2 * h : 2 * h + 2, :], score_v[:, 2 * h : 2 * h + 2, :], EXP, bias=negm[:], accum_out=l_ab[:, h : h + 1])

        v_c = held.tile([P, DV], U32, name="v_c", align_bytes=64)
        v_s = held.tile([P, DV], U8, name="v_s", align_bytes=64)
        nc.vector.quantize_mx(out=v_c[:].bitcast(FP8X4), scales=v_s[:], in_=v_b[:])

        w_b = held.tile([P, NQ, 4], BF16, name="w_b", align_bytes=64)
        w_c = held.tile([P, NQ], U32, name="w_c", align_bytes=64)
        w_s = held.tile([P, NQ], U8, name="w_s", align_bytes=64)
        for h in range(2):
            p_ps = psum.tile([P, 2, NQ], F32, name=f"p_ps{h}")
            for t in range(2):
                nc.tensor.transpose(p_ps[:, t, :], p_sb[:, 2 * h + t, :], ident_f[:])
            for c in ((slice(0, NQ),), (slice(0, NQ // 2), slice(NQ // 2, NQ)))[h]:
                nc.vector.tensor_tensor(
                    w_b[:, c, 2 * h : 2 * h + 2],
                    p_ps[:, :, c].rearrange("s t q -> s q t"),
                    vs_col[:, 2 * h : 2 * h + 2].unsqueeze(1).to_broadcast([P, c.stop - c.start, 2]),
                    MULT,
                )
        for h in range(2):
            c = slice(h * NQ // 2, (h + 1) * NQ // 2)
            nc.vector.quantize_mx(out=w_c[:, c].bitcast(FP8X4), scales=w_s[:, c], in_=w_b[:, c, :].rearrange("p q t -> p (q t)"))

        y_ps = psum.tile([P, DV], F32, name="y_ps")
        nc.tensor.matmul_mx(y_ps[:], lhsT=w_c[:].bitcast(FP8X4), lhsT_scale=w_s[:], rhs=v_c[:].bitcast(FP8X4), rhs_scale=v_s[:], start=True, stop=True)

        e_sink = held.tile([P, 1], F32, name="e_sink")
        nc.scalar.activation(e_sink[:], sink_sb[:], EXP, bias=negm[:])
        l_0 = held.tile([P, 1], F32, name="l_0")
        nc.vector.scalar_tensor_tensor(l_0[:], l_ab[:, 0:1], e_sink[:], l_ab[:, 1:2], ADD, ADD)
        r_l = held.tile([P, 1], F32, name="r_l")
        nc.vector.reciprocal(r_l[:], l_0[:])

        y_sb = held.tile([P, DV], F32, name="y_sb")
        nc.vector.tensor_scalar(y_sb[:], y_ps[:], r_l[:], None, op0=MULT)
        nc.sync.dma_start(out.rearrange("b q e -> (b q) e"), y_sb[:])
